import numpy as np, ml_dtypes
CORES = [9,25,41,57]
N = 4
BF = ml_dtypes.bfloat16
def gentries(a):
    return np.ascontiguousarray(a.reshape(8, 16, -1).transpose(0, 2, 1)).reshape(8, -1)
def gtable(e):
    e = np.asarray(e); return np.ascontiguousarray(e.reshape(8, -1, 16).transpose(0, 2, 1)).reshape(128, -1).astype(np.int32)
W, K, F, O, C, V = 2048, 640, 3, 4, 8, 250
def pick(a, ix):
    return np.take_along_axis(a, ix[:, None, :], 2)
def draw_lists(rng):
    return rng.permuted(np.tile(np.arange(W, dtype=np.int64), (N, 8, N, F, O, 1)), axis=-1)[..., :K].copy()
def frames(rng, T, L, share):
    o = rng.integers(0, O, (N, 8, N, F)); B = np.zeros((N, 8, 16, N, F, K), np.int64)
    for r in range(N):
        for q in range(N):
            for f in range(F):
                v = pick(T[q], L[r, np.arange(8), q, f, o[r, :, q, f]]) + rng.integers(-10, 11, (8, 16, K))
                m = rng.random((8, 16, K)) < share[r, :, q, f][:, None, None]
                B[r, :, :, q, f] = np.clip(np.where(m, v, rng.integers(-V, V + 1, (8, 16, K))), -V, V)
    return B
def pack(R, B, L):
    return {"ref0": np.ascontiguousarray(R.reshape(N, 128, W)).astype(np.float32).astype(BF), "obs": np.ascontiguousarray(B.reshape(N, 128, N * F * K)).astype(np.float32).astype(BF),
            "ops": np.stack([gtable(a.reshape(8, -1)) for a in L])}
def setup_inputs(rng):
    T = rng.integers(-200, 201, (N, 8, 16, W)); R = T + rng.integers(-40, 41, T.shape); L = draw_lists(rng)
    share = rng.choice(np.array([1.0, 0.3, 0.02, 0.0]), (N, 8, N, F))
    return pack(R, frames(rng, T, L, share), L)
def setup_inputs_chain(rng):
    R = rng.integers(-200, 201, (N, 8, 16, W)); L = draw_lists(rng); B = np.zeros((N, 8, 16, N, F, K), np.int64)
    for q in range(N):
        for g in range(8):
            c = rng.permutation(W); P, Q = c[:K], c[K:2 * K]; R[q, g][:, Q] = R[q, g][:, P]
            away = rng.integers(1, 51, (16, K)) * (2 * rng.integers(0, 2, (16, K)) - 1)
            for r in range(N):
                for f in range(F):
                    z = rng.permutation(K); o = rng.permutation(O); e = 1 if rng.random() < 0.7 else -1
                    L[r, g, q, f, o[0]] = P[z]; L[r, g, q, f, o[1]] = Q[z]
                    B[r, g, :, q, f] = (R[q, g][:, P] + e * away)[:, z]
    return pack(R, B, L)
def setup_inputs_edges(rng):
    R = rng.integers(-200, 201, (N, 8, 16, W)); L = draw_lists(rng); B = np.zeros((N, 8, 16, N, F, K), np.int64)
    o = rng.integers(0, O, (N, 8, N, F)); same = rng.random((N, 8, N, F)) < 0.3
    for q in range(N):
        same[q, 0, q, 0] = True; same[q, 1, q, 0] = False
        for r in range(N):
            for f in range(F):
                s = rng.choice(np.array([0, 1, C - 1, C, C + 1, 2 * C]), (8, 16, K)) * (2 * rng.integers(0, 2, (8, 16, K)) - 1)
                B[r, :, :, q, f] = pick(R[q], L[r, np.arange(8), q, f, o[r, :, q, f]]) + np.where(same[r, :, q, f][:, None, None], 0, s)
    return pack(R, B, L)
def setup_inputs_ends(rng):
    R = rng.integers(10, V + 1, (N, 8, 16, W)); L = draw_lists(rng); B = rng.choice(np.array([-V, 1 - V, -1, 0, 1, V - 1, V]), (N, 8, 16, N, F, K))
    runs = [np.arange(K), np.arange(W - K, W), np.arange(K)[::-1], np.arange(W - 1, W - 1 - K, -1), np.arange(K) * (W // K)]
    z = rng.permuted(np.tile(np.arange(8), (N, 1)), axis=1)
    for q in range(N):
        for g in range(8):
            s = 2 * int(rng.integers(0, 2)) - 1; k = int(z[q, g])
            for r in range(N):
                for f in range(F):
                    for o in range(O):
                        i = int(rng.integers(0, len(runs) + 1))
                        L[r, g, q, f, o] = runs[i] if i < len(runs) else np.concatenate([[W - 1], 1 + rng.permutation(W - 2)[:K - 2], [0]])
            if k < 4: R[q, g] = rng.integers(V - 1 if k < 2 else 200, V + 1, (16, W))
            c = rng.permutation(W)
            for t in range(N * F if k % 2 == 1 else 1):
                r, f = (q + t // F) % N, t % F; p1, p2 = c[K - 1 + 2 * t], c[K + 2 * t]
                i = int(rng.integers(0, 16)); a = 259 + (k // 2) % 2 + 4 * int(rng.integers(0, 59)) - V
                R[q, g][:, p2] = R[q, g][:, p1]; R[q, g, i, p1] = a; R[q, g, i, p2] = a + 1
                near = np.append(c[:K - 1], p1); far = np.append(c[:K - 1], p2)
                w = int(rng.integers(1, O))
                if k == 0:
                    w = 1 + 3 * int(rng.integers(0, (O + 1) // 3))
                    if int(np.sum(R[q, g][:, near] + V)) % 2 == 1: R[q, g, 0, c[0]] = 2 * V - 1 - R[q, g, 0, c[0]]
                if k in (2, 3): w = 1 + 2 * int(rng.integers(0, O // 2))
                B[r, g, :, q, f] = -s * V
                for o in range(O): L[r, g, q, f, o] = rng.permutation(near if o == w else far)
            R[q, g] = s * R[q, g]
    return pack(R, B, L)
def setup_inputs_ties(rng):
    s = 2 * rng.integers(0, 2, (N, 8, 16, 1)) - 1; m = rng.integers(N * F * C - V, V - 2 * C, (N, 8, 16, 1))
    R = m + rng.integers(C, 2 * C + 1, (N, 8, 16, W)); R[..., W - 1] = V
    L = np.zeros((N, 8, N, F, O, K), np.int64); B = np.zeros((N, 8, 16, N, F, K), np.int64)
    for q in range(N):
        for g in range(8):
            S = rng.permutation(W - 1)[:K]
            for t in range(N * F):
                r, f = (q + t // F) % N, t % F
                if rng.random() < 0.5: S = rng.permutation(W - 1)[:K]
                w = int(rng.integers(0, O))
                for o in range(O):
                    p = rng.permutation(S)
                    if o < w or (o > w and rng.random() < 0.5): p[rng.integers(0, K)] = W - 1
                    L[r, g, q, f, o] = p
                B[r, g, :, q, f] = s[q, g] * (m[q, g] - t * C + rng.integers(0, C + 1, (16, K)))
    return pack(R * s, B, L)
def setup_inputs_spread(rng):
    z = np.exp2(-rng.integers(0, 9, (N, 8, 1, W)).astype(np.float64))
    T = (rng.integers(-V, V + 1, (N, 8, 16, W)) * z).astype(np.int64); R = np.clip(T + (rng.integers(-60, 61, T.shape) * z).astype(np.int64), -V, V); L = draw_lists(rng)
    share = rng.choice(np.array([1.0, 0.6, 0.1, 0.02, 0.0]), (N, 8, N, F))
    return pack(R, frames(rng, T, L, share), L)
def check_inputs(d):
    bad = []
    for k in ("ref0", "obs"):
        v = np.asarray(d[k]).astype(np.float32)
        if not (np.all(np.abs(v) <= V) and np.all(v == np.rint(v))): bad.append("range of " + k)
    if np.min(d["ops"]) < 0 or np.max(d["ops"]) > W - 1: bad.append("range of ops")
    for a in d["ops"]:
        e = np.sort(gentries(a).reshape(8, -1, K), axis=-1)
        if np.any(e[..., 1:] == e[..., :-1]):
            bad.append("repeated number in a list of ops"); break
    return bad
def reference(ref0, obs, ops):
    R = ref0.astype(np.float32).astype(np.int32).reshape(N, 8, 16, W); x = obs.astype(np.float32).astype(np.int32).reshape(N, 8, 16, N, F, K)
    L = np.stack([gentries(a) for a in ops]).astype(np.int64).reshape(N, 8, N, F, O, K)
    g, i = np.arange(8)[:, None, None], np.arange(16)[None, :, None]
    for q in range(N):
        for d in range(N):
            r = (q + d) % N
            for f in range(F):
                b = x[r, :, :, q, f]
                cost = np.stack([np.sum(np.abs(b - pick(R[q], L[r, :, q, f, o])), axis=(1, 2)) for o in range(O)])
                win = np.argmin(cost, axis=0)
                ix = L[r, np.arange(8), q, f, win]
                v = pick(R[q], ix)
                R[q][g, i, ix[:, None, :]] = v + np.clip(b - v, -C, C)
    return {"y": R.reshape(N, 128, W).astype(np.float32).astype(BF)}

@@ -1,0 +1,224 @@
+from concourse.mybir import AluOpType as ALU, AxisListType as AX, ActivationFunctionType as ACT
+
+N, W, K, F, O, C = 4, 2048, 640, 3, 4, 8
+KC = K // 16
+LC = O * KC
+M = N * F
+PV = 320
+
+SCRATCH = {
+    "rb": ("sbuf", [128, W], "bfloat16"),
+    "rf": ("sbuf", [128, W], "float32"),
+    "bb": ("sbuf", [128, M * K], "bfloat16"),
+    "li": ("sbuf", [128, M * LC], "int32"),
+    "lu": ("sbuf", [128, M * LC], "uint16"),
+    "so": ("sbuf", [128, M * K], "bfloat16"),
+    "sl": ("sbuf", [128, M * LC], "int32"),
+    "dd": ("sbuf", [128, O * K], "float32"),
+    "ab": ("sbuf", [128, O * K], "float32"),
+    "rr": ("sbuf", [128, K], "float32"),
+    "cc": ("sbuf", [128, K], "float32"),
+    "acc": ("sbuf", [128, 4], "float32"),
+    "acv": ("sbuf", [128, 4], "float32"),
+    "mn": ("sbuf", [128, 4], "float32"),
+    "vv": ("sbuf", [128, 4], "float32"),
+    "ww": ("sbuf", [128, 4], "float32"),
+    "w40": ("sbuf", [128, 4], "float32"),
+    "o3": ("sbuf", [128, 8], "uint16"),
+    "o40": ("sbuf", [128, KC], "uint16"),
+    "lw": ("sbuf", [128, 48], "uint16"),
+    "pi": ("sbuf", [128, 4], "int32"),
+    "pj": ("sbuf", [128, 4], "int32"),
+    "pm": ("sbuf", [128, 4], "float32"),
+    "kb": ("sbuf", [128, KC], "float32"),
+    "b40": ("sbuf", [128, KC], "float32"),
+    "b3": ("sbuf", [128, 4], "float32"),
+    "c40": ("sbuf", [128, 4], "float32"),
+    "val": ("sbuf", [128, 128], "float32"),
+    "t1": ("sbuf", [128, 128], "float32"),
+    "t2": ("sbuf", [128, 128], "float32"),
+    "blk": ("sbuf", [128, 128], "float32"),
+    "k1": ("psum", [128, 512], "float32"),
+    "k0": ("psum", [128, 512], "float32"),
+}
+STAGES = [(F, F + 1), (F + 1, 2 * F)] + [(d * F, (d + 1) * F) for d in range(2, N)]
+RELAYED = list(range(F + 1, M, 2))
+SEMAPHORES = (["vs", "ss", "ps", "gs", "ldr", "ldl", "ldb", "ldl2", "ldb1", "ldb2", "cast", "sent", "fed", "stored"]
+              + ["st%d" % i for i in range(len(STAGES))]
+              + ["al%d" % t for t in range(F, M)]
+              + ["ao%d" % t for t in range(F, M)]
+              + ["hp%d" % t for t in RELAYED])
+
+
+def helper_of(c, T, topo):
+    for h in topo.cores_of(c):
+        if topo.die(h) != topo.die(c) and h not in T.cores and all(topo.may_write(h, r) for r in T.cores if r != c):
+            return h
+
+
+def feed_engines(c, T, topo):
+    off = [e for r in T.cores if r != c for e in topo.engines(c, r)]
+    return [e for e in topo.engines(c, helper_of(c, T, topo)) if e not in off]
+
+
+def send_unit(g, T, topo, src, dst, t, to_l, to_o, sem_l, sem_o, local, engines):
+    rid, pid, _ = topo.addr(dst)
+    mask = sum(1 << e for e in engines)
+    g.remote_dma(to_l[:, t * LC:(t + 1) * LC], T.sl[:, t * LC:(t + 1) * LC], sem_l, local, pid, rid, mask)
+    g.remote_dma(to_o[:, t * K:(t + 1) * K], T.so[:, t * K:(t + 1) * K], sem_o, local, pid, rid, mask)
+    return 2 * len(engines)
+
+
+def helper_program(g, core, owner, T, topo):
+    rank, sent = T.rank_of(owner), 0
+    for t in RELAYED:
+        dst = T.cores[(rank - t // F) % N]
+        g.wait_ge(T.sem["hp%d" % t], 2 * len(feed_engines(owner, T, topo)))
+        if sent:
+            g.wait_ge(T.sem.sent, sent)
+        sent += send_unit(g, T, topo, core, dst, t, T.li, T.bb, T.sem["al%d" % t], T.sem["ao%d" % t], T.sem.sent,
+                          topo.engines(core, dst))
+    g.wait_ge(T.sem.sent, sent)
+
+
+def rank_program(g, core, T, topo):
+    rank = T.rank_of(core)
+    if rank is None:
+        for c in T.cores:
+            if helper_of(c, T, topo) == core:
+                helper_program(g, core, c, T, topo)
+        return
+    V, S, P, Y, sem = g.vector, g.scalar, g.tensor, g.sync, T.sem
+    n = {"vs": 0, "ss": 0, "ps": 0, "gs": 0}
+
+    def mark(ins, name):
+        ins.then_inc(sem[name], 1)
+        n[name] += 1
+        return n[name]
+
+    def v(ins):
+        return mark(ins, "vs")
+
+    def vwait(k):
+        V.wait_ge(sem.vs, k)
+
+    ob, ol = rank * F * K, rank * F * LC
+
+    Y.dma_start(T.rb[:], T.ref0[:]).then_inc(sem.ldr, 16)
+    S.dma_start(T.li[:, 0:LC], T.ops[:, ol:ol + LC]).then_inc(sem.ldl, 16)
+    S.dma_start(T.bb[:, 0:K], T.obs[:, ob:ob + K]).then_inc(sem.ldb, 16)
+    Y.wait_ge(sem.ldr, 16)
+    Y.dma_start(T.bb[:, K:2 * K], T.obs[:, ob + K:ob + 2 * K]).then_inc(sem.ldb1, 16)
+    Y.wait_ge(sem.cast, 16)
+    for i, (t0, t1) in enumerate(STAGES):
+        d = t0 // F
+        u = ((rank - d) % N - d) * F
+        Y.dma_start(T.sl[:, t0 * LC:t1 * LC], T.ops[:, (u + t0) * LC:(u + t1) * LC]).then_inc(sem["st%d" % i], 16)
+        Y.dma_start(T.so[:, t0 * K:t1 * K], T.obs[:, (u + t0) * K:(u + t1) * K]).then_inc(sem["st%d" % i], 16)
+        if i == 0:
+            Y.dma_start(T.bb[:, 2 * K:F * K], T.obs[:, ob + 2 * K:ob + F * K]).then_inc(sem.ldb2, 16)
+        if i < len(STAGES) - 1:
+            Y.wait_ge(sem["st%d" % i], 32)
+
+    mark(g.iota(T.pi[:, 0:1], [[0, 1]], 0, 1), "gs")
+    mark(g.iota(T.kb[:], [[1, KC]], 0, 0, allow_small_or_imprecise_dtypes=True), "gs")
+    mark(g.iota(T.val[:], [[16, 8], [0, 16]], 0, -1, allow_small_or_imprecise_dtypes=True), "gs")
+    g.dma_start(T.li[:, LC:F * LC], T.ops[:, ol + LC:ol + F * LC]).then_inc(sem.ldl2, 16)
+    g.wait_ge(sem.ldr, 16)
+    g.dma_start(T.rf[:], T.rb[:]).then_inc(sem.cast, 16)
+    helper = helper_of(core, T, topo)
+    sent = fed = 0
+    for i, (t0, t1) in enumerate(STAGES):
+        g.wait_ge(sem["st%d" % i], 32)
+        for t in range(t0, t1):
+            if t in RELAYED:
+                fed += send_unit(g, T, topo, core, helper, t, T.sl, T.so, sem["hp%d" % t], sem["hp%d" % t], sem.fed,
+                                 feed_engines(core, T, topo))
+        for t in range(t0, t1):
+            if t not in RELAYED:
+                dst = T.cores[(rank - t // F) % N]
+                if sent:
+                    g.wait_ge(sem.sent, sent)
+                sent += send_unit(g, T, topo, core, dst, t, T.li, T.bb, sem["al%d" % t], sem["ao%d" % t], sem.sent,
+                                  topo.engines(core, dst))
+
+    def arrivals(t):
+        src = T.cores[(rank + t // F) % N]
+        return len(topo.engines(helper_of(src, T, topo) if t in RELAYED else src, core))
+
+    v(V.memset(T.vv[:], 1.0e6))
+    v(V.memset(T.c40[:], float(KC)))
+    V.wait_ge(sem.gs, 3)
+    a = v(V.tensor_scalar(T.pj[:, 0:1], T.pi[:, 0:1], 15, None, ALU.bitwise_and))
+    v(V.tensor_scalar(T.t1[:], T.val[:], -16.0, None, ALU.is_gt))
+    b = v(V.tensor_scalar(T.t2[:], T.val[:], 0.0, None, ALU.is_le))
+    vwait(a)
+    a = v(V.tensor_scalar(T.pm[:, 0:1], T.pj[:, 0:1], 1.0 / 16, None, ALU.mult))
+    vwait(b)
+    v(V.tensor_tensor(T.blk[:], T.t1[:], T.t2[:], ALU.mult))
+    vwait(a)
+    a = v(V.tensor_scalar(T.b40[:], T.kb[:], T.pm[:, 0:1], None, ALU.add))
+    vwait(a)
+    v(V.tensor_scalar(T.b3[:], T.b40[:, 0:4], 16.0, float(KC - 1), ALU.mult, ALU.min))
+    V.wait_ge(sem.ldl, 16)
+    last = v(V.tensor_copy(T.lu[:, 0:LC], T.li[:, 0:LC]))
+    V.wait_ge(sem.ldr, 16)
+
+    for t in range(M):
+        R = T.rb if t == 0 else T.rf
+        bt = T.bb[:, t * K:(t + 1) * K]
+        if t < F:
+            V.wait_ge(sem[("ldb", "ldb1", "ldb2")[t]], 16)
+        else:
+            V.wait_ge(sem["ao%d" % t], arrivals(t))
+        vwait(last)
+        sa = []
+        for i, o in enumerate(range(O - 1, -1, -1)):
+            c0 = t * LC + o * KC
+            gk = v(V.tensor_tensor(T.dd[:, o * K:(o + 1) * K], R[:, 0:W].indirect(T.lu[:, c0:c0 + KC]), bt, ALU.subtract))
+            hi = (o + 1) * K - (PV if o == 0 else 0)
+            S.wait_ge(sem.vs, gk)
+            sa.append(mark(S.activation(T.ab[:, o * K:hi], T.dd[:, o * K:hi], ACT.Abs, accum_out=T.acc[:, i:i + 1]), "ss"))
+        vwait(gk)
+        rv = v(V.tensor_reduce(T.acv[:, 0:1], T.dd[:, K - PV:K], AX.X, ALU.add, apply_absolute_value=True))
+        P.wait_ge(sem.ss, sa[2])
+        p1 = mark(P.matmul(T.k1[:, 0:3], T.blk[:], T.acc[:, 0:3], True, True), "ps")
+        P.wait_ge(sem.vs, rv)
+        P.matmul(T.k0[:, 0:1], T.blk[:], T.acv[:, 0:1], True, False)
+        P.wait_ge(sem.ss, sa[3])
+        p0 = mark(P.matmul(T.k0[:, 0:1], T.blk[:], T.acc[:, 3:4], False, True), "ps")
+        V.wait_ge(sem.ps, p1)
+        a = v(V.tensor_reduce(T.mn[:, 0:1], T.k1[:, 0:3], AX.X, ALU.min))
+        if t + 1 < M:
+            if t == 0:
+                V.wait_ge(sem.ldl2, 16)
+            elif t + 1 >= F:
+                V.wait_ge(sem["al%d" % (t + 1)], arrivals(t + 1))
+            v(V.tensor_copy(T.lu[:, (t + 1) * LC:(t + 2) * LC], T.li[:, (t + 1) * LC:(t + 2) * LC]))
+        vwait(a)
+        a = v(V.tensor_scalar(T.vv[:, 0:2], T.k1[:, 1:3], T.mn[:, 0:1], 128.0, ALU.subtract, ALU.mult))
+        vwait(a)
+        a = v(V.tensor_tensor_scan(T.ww[:, 0:3], T.c40[:, 0:3], T.vv[:, 0:3], 0.0, ALU.add, ALU.min))
+        vwait(a)
+        V.wait_ge(sem.ps, p0)
+        a = v(V.tensor_scalar(T.w40[:, 0:1], T.k0[:, 0:1], T.mn[:, 0:1], T.ww[:, 2:3], ALU.is_gt, ALU.mult))
+        vwait(a)
+        a = v(V.tensor_scalar(T.o3[:, 0:3], T.b3[:, 0:3], T.w40[:, 0:1], None, ALU.add))
+        vwait(a)
+        e = v(V.tensor_copy(T.lw[:], T.li[:, t * LC:(t + 1) * LC].indirect(T.o3[:, 0:3])))
+        a = v(V.tensor_scalar(T.o40[:], T.b40[:], T.w40[:, 0:1], 16.0, ALU.add, ALU.mult))
+        vwait(a)
+        a = v(V.tensor_scalar(T.cc[:], T.dd[:, 0:O * K].indirect(T.o40[:, 0:KC]), float(-C), float(C), ALU.max, ALU.min))
+        S.wait_ge(sem.vs, e)
+        sr = mark(S.activation(T.rr[:], R[:, 0:W].indirect(T.lw[:, 0:KC]), ACT.Identity), "ss")
+        if t == 0:
+            V.wait_ge(sem.cast, 16)
+        vwait(a)
+        V.wait_ge(sem.ss, sr)
+        last = v(V.tensor_tensor(T.rf[:, 0:W].indirect(T.lw[:, 0:KC]), T.rr[:], T.cc[:], ALU.subtract))
+
+    g.wait_ge(sem.sent, sent)
+    g.wait_ge(sem.fed, fed)
+    g.wait_ge(sem.vs, last)
+    g.dma_start(T.y[:], T.rf[:]).then_inc(sem.stored, 16)
+    g.wait_ge(sem.stored, 16)

@@ -4,7 +4,8 @@ N, W, K, F, O, C = 4, 2048, 640, 3, 4, 8
 KC = K // 16
 LC = O * KC
 M = N * F
-PV = 320
+BANK = 512
+MID = -160000.0
 
 SCRATCH = {
     "rb": ("sbuf", [128, W], "bfloat16"),
@@ -12,17 +13,17 @@ SCRATCH = {
     "bb": ("sbuf", [128, M * K], "bfloat16"),
     "li": ("sbuf", [128, M * LC], "int32"),
     "lu": ("sbuf", [128, M * LC], "uint16"),
+    "lx": ("sbuf", [128, LC], "int32"),
     "so": ("sbuf", [128, M * K], "bfloat16"),
     "sl": ("sbuf", [128, M * LC], "int32"),
     "dd": ("sbuf", [128, O * K], "float32"),
     "ab": ("sbuf", [128, O * K], "float32"),
+    "r3": ("sbuf", [128, K], "bfloat16"),
     "rr": ("sbuf", [128, K], "float32"),
     "cc": ("sbuf", [128, K], "float32"),
     "acc": ("sbuf", [128, 4], "float32"),
-    "acv": ("sbuf", [128, 4], "float32"),
     "mn": ("sbuf", [128, 4], "float32"),
-    "vv": ("sbuf", [128, 4], "float32"),
-    "ww": ("sbuf", [128, 4], "float32"),
+    "m1": ("sbuf", [128, 4], "float32"),
     "w40": ("sbuf", [128, 4], "float32"),
     "o3": ("sbuf", [128, 8], "uint16"),
     "o40": ("sbuf", [128, KC], "uint16"),
@@ -33,13 +34,16 @@ SCRATCH = {
     "kb": ("sbuf", [128, KC], "float32"),
     "b40": ("sbuf", [128, KC], "float32"),
     "b3": ("sbuf", [128, 4], "float32"),
-    "c40": ("sbuf", [128, 4], "float32"),
-    "val": ("sbuf", [128, 128], "float32"),
-    "t1": ("sbuf", [128, 128], "float32"),
-    "t2": ("sbuf", [128, 128], "float32"),
+    "px": ("sbuf", [128, 16], "float32"),
+    "pe": ("sbuf", [128, 16], "uint16"),
+    "one": ("sbuf", [128, 4], "float32"),
+    "mid": ("sbuf", [128, 4], "float32"),
+    "dia": ("sbuf", [128, 128], "float32"),
     "blk": ("sbuf", [128, 128], "float32"),
-    "k1": ("psum", [128, 512], "float32"),
-    "k0": ("psum", [128, 512], "float32"),
+    "idp": ("sbuf", [128, 128], "bfloat16"),
+    "idn": ("sbuf", [128, 128], "bfloat16"),
+    "pd": ("psum", [128, 2 * BANK], "float32"),
+    "key": ("psum", [128, BANK], "float32"),
 }
 STAGES = [(F, F + 1), (F + 1, 2 * F)] + [(d * F, (d + 1) * F) for d in range(2, N)]
 RELAYED = list(range(F + 1, M, 2))
@@ -122,8 +126,13 @@ def rank_program(g, core, T, topo):
 
     mark(g.iota(T.pi[:, 0:1], [[0, 1]], 0, 1), "gs")
     mark(g.iota(T.kb[:], [[1, KC]], 0, 0, allow_small_or_imprecise_dtypes=True), "gs")
-    mark(g.iota(T.val[:], [[16, 8], [0, 16]], 0, -1, allow_small_or_imprecise_dtypes=True), "gs")
+    mark(g.iota(T.dia[:], [[-1, 128]], 0, 1, allow_small_or_imprecise_dtypes=True), "gs")
+    a = mark(g.iota(T.blk[:], [[0, 128]], 4, 0, allow_small_or_imprecise_dtypes=True), "gs")
     g.dma_start(T.li[:, LC:F * LC], T.ops[:, ol + LC:ol + F * LC]).then_inc(sem.ldl2, 16)
+    g.wait_ge(sem.gs, a)
+    a = mark(g.affine_select(T.blk[:], T.blk[:], [[16, 8], [0, 16]], ALU.is_gt, 0.0, 16, -1), "gs")
+    g.wait_ge(sem.gs, a)
+    block = mark(g.affine_select(T.blk[:], T.blk[:], [[-16, 8], [0, 16]], ALU.is_ge, 0.0, 0, 1), "gs")
     g.wait_ge(sem.ldr, 16)
     g.dma_start(T.rf[:], T.rb[:]).then_inc(sem.cast, 16)
     helper = helper_of(core, T, topo)
@@ -146,68 +155,95 @@ def rank_program(g, core, T, topo):
         src = T.cores[(rank + t // F) % N]
         return len(topo.engines(helper_of(src, T, topo) if t in RELAYED else src, core))
 
-    v(V.memset(T.vv[:], 1.0e6))
-    v(V.memset(T.c40[:], float(KC)))
+    def frame_wait(Q, t):
+        if t < F:
+            Q.wait_ge(sem[("ldb", "ldb1", "ldb2")[t]], 16)
+        else:
+            Q.wait_ge(sem["ao%d" % t], arrivals(t))
+
+    v(V.memset(T.one[:], 1.0))
+    v(V.memset(T.mid[:], MID))
+    V.wait_ge(sem.gs, 1)
+    v(V.tensor_scalar(T.pj[:, 0:1], T.pi[:, 0:1], 15, None, ALU.bitwise_and))
+    v(V.tensor_scalar(T.pj[:, 1:2], T.pi[:, 0:1], 3, None, ALU.bitwise_and))
+    a = v(V.tensor_scalar(T.pj[:, 2:3], T.pi[:, 0:1], 15, 2, ALU.bitwise_and, ALU.logical_shift_right))
+    vwait(a)
+    v(V.tensor_scalar(T.pm[:, 0:1], T.pj[:, 0:1], 1.0 / 16, None, ALU.mult))
+    v(V.tensor_scalar(T.pm[:, 1:2], T.pj[:, 1:2], float(KC), None, ALU.mult))
+    a = v(V.tensor_copy(T.pm[:, 2:3], T.pj[:, 2:3]))
+    vwait(a)
     V.wait_ge(sem.gs, 3)
-    a = v(V.tensor_scalar(T.pj[:, 0:1], T.pi[:, 0:1], 15, None, ALU.bitwise_and))
-    v(V.tensor_scalar(T.t1[:], T.val[:], -16.0, None, ALU.is_gt))
-    b = v(V.tensor_scalar(T.t2[:], T.val[:], 0.0, None, ALU.is_le))
+    v(V.tensor_scalar(T.b40[:], T.kb[:], T.pm[:, 0:1], None, ALU.add))
+    a = v(V.tensor_scalar(T.px[:], T.kb[:, 0:16], 4.0, T.pm[:, 1:2], ALU.mult, ALU.add))
+    v(V.tensor_scalar(T.idn[:], T.dia[:], 0.0, -1.0, ALU.is_equal, ALU.mult))
+    v(V.tensor_scalar(T.idp[:], T.dia[:], 0.0, None, ALU.is_equal))
     vwait(a)
-    a = v(V.tensor_scalar(T.pm[:, 0:1], T.pj[:, 0:1], 1.0 / 16, None, ALU.mult))
-    vwait(b)
-    v(V.tensor_tensor(T.blk[:], T.t1[:], T.t2[:], ALU.mult))
-    vwait(a)
-    a = v(V.tensor_scalar(T.b40[:], T.kb[:], T.pm[:, 0:1], None, ALU.add))
-    vwait(a)
-    v(V.tensor_scalar(T.b3[:], T.b40[:, 0:4], 16.0, float(KC - 1), ALU.mult, ALU.min))
+    v(V.tensor_scalar(T.b3[:], T.b40[:, 0:4], 64.0, 4.0 * (KC - 1), ALU.mult, ALU.min))
+    consts = v(V.tensor_scalar(T.pe[:], T.px[:], T.pm[:, 2:3], None, ALU.add))
     V.wait_ge(sem.ldl, 16)
     last = v(V.tensor_copy(T.lu[:, 0:LC], T.li[:, 0:LC]))
     V.wait_ge(sem.ldr, 16)
+    S.wait_ge(sem.ldr, 16)
+    P.wait_ge(sem.vs, consts)
+    P.wait_ge(sem.gs, block)
+    copied = 0
+    parts = [(0, BANK), (BANK, K)]
 
     for t in range(M):
         R = T.rb if t == 0 else T.rf
         bt = T.bb[:, t * K:(t + 1) * K]
-        if t < F:
-            V.wait_ge(sem[("ldb", "ldb1", "ldb2")[t]], 16)
-        else:
-            V.wait_ge(sem["ao%d" % t], arrivals(t))
+
+        def way(o):
+            return R[:, 0:W].indirect(T.lu[:, t * LC + o * KC:t * LC + (o + 1) * KC])
+
+        def sum_abs(o, src):
+            return mark(S.activation(T.ab[:, o * K:(o + 1) * K], src, ACT.Abs, accum_out=T.acc[:, 3 - o:4 - o]), "ss")
+
+        S.wait_ge(sem.vs, last)
+        s3 = mark(S.activation(T.r3[:], way(3), ACT.Identity), "ss")
+        frame_wait(P, t)
+        if copied:
+            P.wait_ge(sem.ss, copied)
+        for a0, a1 in parts:
+            P.matmul(T.pd[:, a0:a1], T.idn[:], T.bb[:, t * K + a0:t * K + a1], True, False)
+        P.wait_ge(sem.ss, s3)
+        for a0, a1 in parts:
+            p3 = mark(P.matmul(T.pd[:, a0:a1], T.idp[:], T.r3[:, a0:a1], False, True), "ps")
+        P.matmul(T.key[:, 0:O], T.blk[:], T.mid[:], True, False)
+        frame_wait(V, t)
         vwait(last)
-        sa = []
-        for i, o in enumerate(range(O - 1, -1, -1)):
-            c0 = t * LC + o * KC
-            gk = v(V.tensor_tensor(T.dd[:, o * K:(o + 1) * K], R[:, 0:W].indirect(T.lu[:, c0:c0 + KC]), bt, ALU.subtract))
-            hi = (o + 1) * K - (PV if o == 0 else 0)
-            S.wait_ge(sem.vs, gk)
-            sa.append(mark(S.activation(T.ab[:, o * K:hi], T.dd[:, o * K:hi], ACT.Abs, accum_out=T.acc[:, i:i + 1]), "ss"))
-        vwait(gk)
-        rv = v(V.tensor_reduce(T.acv[:, 0:1], T.dd[:, K - PV:K], AX.X, ALU.add, apply_absolute_value=True))
-        P.wait_ge(sem.ss, sa[2])
-        p1 = mark(P.matmul(T.k1[:, 0:3], T.blk[:], T.acc[:, 0:3], True, True), "ps")
+        gk = {o: v(V.tensor_tensor(T.dd[:, o * K:(o + 1) * K], way(o), bt, ALU.subtract)) for o in (2, 1, 0)}
+        S.wait_ge(sem.vs, gk[2])
+        sum_abs(2, T.dd[:, 2 * K:3 * K])
+        S.wait_ge(sem.ps, p3)
+        sum_abs(3, T.pd[:, 0:K])
+        S.wait_ge(sem.vs, gk[1])
+        s1 = sum_abs(1, T.dd[:, K:2 * K])
+        copied = mark(S.activation(T.dd[:, 3 * K:4 * K], T.pd[:, 0:K], ACT.Identity), "ss")
+        vwait(gk[0])
+        rv = v(V.tensor_reduce(T.acc[:, 3:4], T.dd[:, 0:K], AX.X, ALU.add, apply_absolute_value=True))
+        P.wait_ge(sem.ss, s1)
         P.wait_ge(sem.vs, rv)
-        P.matmul(T.k0[:, 0:1], T.blk[:], T.acv[:, 0:1], True, False)
-        P.wait_ge(sem.ss, sa[3])
-        p0 = mark(P.matmul(T.k0[:, 0:1], T.blk[:], T.acc[:, 3:4], False, True), "ps")
-        V.wait_ge(sem.ps, p1)
-        a = v(V.tensor_reduce(T.mn[:, 0:1], T.k1[:, 0:3], AX.X, ALU.min))
+        pk = mark(P.matmul(T.key[:, 0:O], T.blk[:], T.acc[:], False, True), "ps")
+        v(V.tensor_copy(T.lx[:], T.li[:, t * LC:(t + 1) * LC].indirect(T.pe[:, 0:LC // 16])))
         if t + 1 < M:
             if t == 0:
                 V.wait_ge(sem.ldl2, 16)
             elif t + 1 >= F:
                 V.wait_ge(sem["al%d" % (t + 1)], arrivals(t + 1))
             v(V.tensor_copy(T.lu[:, (t + 1) * LC:(t + 2) * LC], T.li[:, (t + 1) * LC:(t + 2) * LC]))
+        V.wait_ge(sem.ps, pk)
+        v(V.tensor_tensor_scan(T.m1[:], T.one[:], T.key[:, 0:O], 1.0e9, ALU.add, ALU.min))
+        a = v(V.tensor_reduce(T.mn[:, 0:1], T.key[:, 0:O], AX.X, ALU.min))
         vwait(a)
-        a = v(V.tensor_scalar(T.vv[:, 0:2], T.k1[:, 1:3], T.mn[:, 0:1], 128.0, ALU.subtract, ALU.mult))
+        a = v(V.tensor_scalar(T.o3[:, 0:3], T.b3[:, 0:3], T.m1[:, 3:4], T.mn[:, 0:1], ALU.add, ALU.subtract))
+        b = v(V.tensor_scalar(T.w40[:, 0:1], T.m1[:, 3:4], T.mn[:, 0:1], float(KC), ALU.subtract, ALU.mult))
         vwait(a)
-        a = v(V.tensor_tensor_scan(T.ww[:, 0:3], T.c40[:, 0:3], T.vv[:, 0:3], 0.0, ALU.add, ALU.min))
-        vwait(a)
-        V.wait_ge(sem.ps, p0)
-        a = v(V.tensor_scalar(T.w40[:, 0:1], T.k0[:, 0:1], T.mn[:, 0:1], T.ww[:, 2:3], ALU.is_gt, ALU.mult))
-        vwait(a)
-        a = v(V.tensor_scalar(T.o3[:, 0:3], T.b3[:, 0:3], T.w40[:, 0:1], None, ALU.add))
-        vwait(a)
-        e = v(V.tensor_copy(T.lw[:], T.li[:, t * LC:(t + 1) * LC].indirect(T.o3[:, 0:3])))
+        e = v(V.tensor_copy(T.lw[:], T.lx[:, 0:LC].indirect(T.o3[:, 0:3])))
+        vwait(b)
         a = v(V.tensor_scalar(T.o40[:], T.b40[:], T.w40[:, 0:1], 16.0, ALU.add, ALU.mult))
         vwait(a)
+        V.wait_ge(sem.ss, copied)
         a = v(V.tensor_scalar(T.cc[:], T.dd[:, 0:O * K].indirect(T.o40[:, 0:KC]), float(-C), float(C), ALU.max, ALU.min))
         S.wait_ge(sem.vs, e)
         sr = mark(S.activation(T.rr[:], R[:, 0:W].indirect(T.lw[:, 0:KC]), ACT.Identity), "ss")

@@ -5,49 +5,57 @@ KC = K // 16
 LC = O * KC
 M = N * F
 BANK = 512
+H = K // 2
+HC = H // 16
+SLOTS = [3, 0, 1, 2, 3]
+NS = len(SLOTS)
+LW = 64
+LX = LW * NS
+LATE = 96
+GW = 1280
+BIG = 3.0 * 2 ** 24
 MID = -160000.0
 
 SCRATCH = {
     "rb": ("sbuf", [128, W], "bfloat16"),
     "rf": ("sbuf", [128, W], "float32"),
     "bb": ("sbuf", [128, M * K], "bfloat16"),
-    "li": ("sbuf", [128, M * LC], "int32"),
+    "li": ("sbuf", [128, M * O, KC], "int32"),
     "lu": ("sbuf", [128, M * LC], "uint16"),
-    "lx": ("sbuf", [128, LC], "int32"),
+    "lx": ("sbuf", [128, 2 * LX], "int32"),
     "so": ("sbuf", [128, M * K], "bfloat16"),
-    "sl": ("sbuf", [128, M * LC], "int32"),
-    "dd": ("sbuf", [128, O * K], "float32"),
-    "ab": ("sbuf", [128, O * K], "float32"),
-    "r3": ("sbuf", [128, K], "bfloat16"),
+    "sl": ("sbuf", [128, M * O, KC], "int32"),
+    "dd": ("sbuf", [128, O * H], "float32"),
+    "rs": ("sbuf", [128, O * H], "bfloat16"),
+    "t1": ("sbuf", [128, O * H], "float32"),
+    "ab": ("sbuf", [128, O * H], "float32"),
     "rr": ("sbuf", [128, K], "float32"),
     "cc": ("sbuf", [128, K], "float32"),
-    "acc": ("sbuf", [128, 4], "float32"),
-    "mn": ("sbuf", [128, 4], "float32"),
-    "m1": ("sbuf", [128, 4], "float32"),
-    "w40": ("sbuf", [128, 4], "float32"),
+    "rq": ("sbuf", [128, K], "bfloat16"),
+    "cq": ("sbuf", [128, K], "bfloat16"),
+    "tq": ("sbuf", [128, H], "bfloat16"),
+    "ac1": ("sbuf", [128, 8], "float32"),
+    "ac2": ("sbuf", [128, 8], "float32"),
+    "m1": ("sbuf", [128, 8], "float32"),
     "o3": ("sbuf", [128, 8], "uint16"),
-    "o40": ("sbuf", [128, KC], "uint16"),
-    "lw": ("sbuf", [128, 48], "uint16"),
+    "lw": ("sbuf", [128, LW], "uint16"),
     "pi": ("sbuf", [128, 4], "int32"),
     "pj": ("sbuf", [128, 4], "int32"),
     "pm": ("sbuf", [128, 4], "float32"),
-    "kb": ("sbuf", [128, KC], "float32"),
-    "b40": ("sbuf", [128, KC], "float32"),
+    "kd": ("sbuf", [128, LX - KC * NS], "float32"),
     "b3": ("sbuf", [128, 4], "float32"),
-    "px": ("sbuf", [128, 16], "float32"),
-    "pe": ("sbuf", [128, 16], "uint16"),
-    "one": ("sbuf", [128, 4], "float32"),
-    "mid": ("sbuf", [128, 4], "float32"),
+    "one": ("sbuf", [128, 8], "float32"),
+    "mid": ("sbuf", [128, 8], "float32"),
     "dia": ("sbuf", [128, 128], "float32"),
     "blk": ("sbuf", [128, 128], "float32"),
     "idp": ("sbuf", [128, 128], "bfloat16"),
     "idn": ("sbuf", [128, 128], "bfloat16"),
-    "pd": ("psum", [128, 2 * BANK], "float32"),
+    "pd": ("psum", [128, O * BANK], "float32"),
     "key": ("psum", [128, BANK], "float32"),
 }
 STAGES = [(F, F + 1), (F + 1, 2 * F)] + [(d * F, (d + 1) * F) for d in range(2, N)]
 RELAYED = list(range(F + 1, M, 2))
-SEMAPHORES = (["vs", "ss", "ps", "gs", "ldr", "ldl", "ldb", "ldl2", "ldb1", "ldb2", "cast", "sent", "fed", "stored"]
+SEMAPHORES = (["vs", "ss", "ps", "gs", "ldr", "ldl", "ldb", "ldl2", "ldb1", "ldb2", "cast", "wide", "sent", "fed", "stored"]
               + ["st%d" % i for i in range(len(STAGES))]
               + ["al%d" % t for t in range(F, M)]
               + ["ao%d" % t for t in range(F, M)]
@@ -68,7 +76,7 @@ def feed_engines(c, T, topo):
 def send_unit(g, T, topo, src, dst, t, to_l, to_o, sem_l, sem_o, local, engines):
     rid, pid, _ = topo.addr(dst)
     mask = sum(1 << e for e in engines)
-    g.remote_dma(to_l[:, t * LC:(t + 1) * LC], T.sl[:, t * LC:(t + 1) * LC], sem_l, local, pid, rid, mask)
+    g.remote_dma(to_l[:, t * O:(t + 1) * O], T.sl[:, t * O:(t + 1) * O], sem_l, local, pid, rid, mask)
     g.remote_dma(to_o[:, t * K:(t + 1) * K], T.so[:, t * K:(t + 1) * K], sem_o, local, pid, rid, mask)
     return 2 * len(engines)
 
@@ -103,21 +111,23 @@ def rank_program(g, core, T, topo):
     def v(ins):
         return mark(ins, "vs")
 
+    def s(ins):
+        return mark(ins, "ss")
+
     def vwait(k):
         V.wait_ge(sem.vs, k)
 
     ob, ol = rank * F * K, rank * F * LC
 
     Y.dma_start(T.rb[:], T.ref0[:]).then_inc(sem.ldr, 16)
-    S.dma_start(T.li[:, 0:LC], T.ops[:, ol:ol + LC]).then_inc(sem.ldl, 16)
+    S.dma_start(T.li[:, 0:O], T.ops[:, ol:ol + LC]).then_inc(sem.ldl, 16)
     S.dma_start(T.bb[:, 0:K], T.obs[:, ob:ob + K]).then_inc(sem.ldb, 16)
     Y.wait_ge(sem.ldr, 16)
     Y.dma_start(T.bb[:, K:2 * K], T.obs[:, ob + K:ob + 2 * K]).then_inc(sem.ldb1, 16)
-    Y.wait_ge(sem.cast, 16)
     for i, (t0, t1) in enumerate(STAGES):
         d = t0 // F
         u = ((rank - d) % N - d) * F
-        Y.dma_start(T.sl[:, t0 * LC:t1 * LC], T.ops[:, (u + t0) * LC:(u + t1) * LC]).then_inc(sem["st%d" % i], 16)
+        Y.dma_start(T.sl[:, t0 * O:t1 * O], T.ops[:, (u + t0) * LC:(u + t1) * LC]).then_inc(sem["st%d" % i], 16)
         Y.dma_start(T.so[:, t0 * K:t1 * K], T.obs[:, (u + t0) * K:(u + t1) * K]).then_inc(sem["st%d" % i], 16)
         if i == 0:
             Y.dma_start(T.bb[:, 2 * K:F * K], T.obs[:, ob + 2 * K:ob + F * K]).then_inc(sem.ldb2, 16)
@@ -125,16 +135,17 @@ def rank_program(g, core, T, topo):
             Y.wait_ge(sem["st%d" % i], 32)
 
     mark(g.iota(T.pi[:, 0:1], [[0, 1]], 0, 1), "gs")
-    mark(g.iota(T.kb[:], [[1, KC]], 0, 0, allow_small_or_imprecise_dtypes=True), "gs")
+    mark(g.iota(T.kd[:], [[16, LW - KC], [H, NS]], -H, 0, allow_small_or_imprecise_dtypes=True), "gs")
     mark(g.iota(T.dia[:], [[-1, 128]], 0, 1, allow_small_or_imprecise_dtypes=True), "gs")
     a = mark(g.iota(T.blk[:], [[0, 128]], 4, 0, allow_small_or_imprecise_dtypes=True), "gs")
-    g.dma_start(T.li[:, LC:F * LC], T.ops[:, ol + LC:ol + F * LC]).then_inc(sem.ldl2, 16)
+    g.dma_start(T.li[:, O:F * O], T.ops[:, ol + LC:ol + F * LC]).then_inc(sem.ldl2, 16)
     g.wait_ge(sem.gs, a)
     a = mark(g.affine_select(T.blk[:], T.blk[:], [[16, 8], [0, 16]], ALU.is_gt, 0.0, 16, -1), "gs")
     g.wait_ge(sem.gs, a)
     block = mark(g.affine_select(T.blk[:], T.blk[:], [[-16, 8], [0, 16]], ALU.is_ge, 0.0, 0, 1), "gs")
+    g.dma_start(T.rf[:, GW:W], T.ref0[:, GW:W]).then_inc(sem.cast, 16)
     g.wait_ge(sem.ldr, 16)
-    g.dma_start(T.rf[:], T.rb[:]).then_inc(sem.cast, 16)
+    g.affine_select(T.rf[:, 0:GW], T.rb[:, 0:GW], [[0, GW]], ALU.is_ge, 0.0, 0, 0).then_inc(sem.wide, 1)
     helper = helper_of(core, T, topo)
     sent = fed = 0
     for i, (t0, t1) in enumerate(STAGES):
@@ -161,100 +172,163 @@ def rank_program(g, core, T, topo):
         else:
             Q.wait_ge(sem["ao%d" % t], arrivals(t))
 
-    v(V.memset(T.one[:], 1.0))
-    v(V.memset(T.mid[:], MID))
+    def lists_wait(t):
+        if t < 2:
+            V.wait_ge(sem[("ldl", "ldl2")[t]], 16)
+        elif t >= F:
+            V.wait_ge(sem["al%d" % t], arrivals(t))
+
+    def offsets(t, h):
+        if t < M:
+            c0 = t * LC + h * O * HC
+            return v(V.tensor_copy(T.lu[:, c0:c0 + O * HC], T.li[:, t * O:(t + 1) * O, h * HC:(h + 1) * HC]))
+
+    def table(t, i):
+        if t < M:
+            c0 = t % 2 * LX
+            return v(V.tensor_copy(T.lx[:, c0 + i:c0 + KC * NS:NS], T.li[:, t * O + SLOTS[i]]))
+
+    for c0, c1, step in ((0, 4, 1.0), (4, 5, -1.0), (5, 6, BIG), (6, 8, -BIG)):
+        v(V.memset(T.one[:, c0:c1], step))
+    v(V.memset(T.mid[:, 0:4], MID))
+    v(V.memset(T.mid[:, 4:8], BIG))
+    v(V.memset(T.ac1[:], 0.0))
+    v(V.memset(T.ac2[:], 0.0))
     V.wait_ge(sem.gs, 1)
-    v(V.tensor_scalar(T.pj[:, 0:1], T.pi[:, 0:1], 15, None, ALU.bitwise_and))
-    v(V.tensor_scalar(T.pj[:, 1:2], T.pi[:, 0:1], 3, None, ALU.bitwise_and))
-    a = v(V.tensor_scalar(T.pj[:, 2:3], T.pi[:, 0:1], 15, 2, ALU.bitwise_and, ALU.logical_shift_right))
+    a = v(V.tensor_scalar(T.pj[:, 0:1], T.pi[:, 0:1], 15, None, ALU.bitwise_and))
     vwait(a)
-    v(V.tensor_scalar(T.pm[:, 0:1], T.pj[:, 0:1], 1.0 / 16, None, ALU.mult))
-    v(V.tensor_scalar(T.pm[:, 1:2], T.pj[:, 1:2], float(KC), None, ALU.mult))
-    a = v(V.tensor_copy(T.pm[:, 2:3], T.pj[:, 2:3]))
+    a = v(V.tensor_copy(T.pm[:, 0:1], T.pj[:, 0:1]))
     vwait(a)
     V.wait_ge(sem.gs, 3)
-    v(V.tensor_scalar(T.b40[:], T.kb[:], T.pm[:, 0:1], None, ALU.add))
-    a = v(V.tensor_scalar(T.px[:], T.kb[:, 0:16], 4.0, T.pm[:, 1:2], ALU.mult, ALU.add))
+    v(V.tensor_scalar(T.kd[:, 0::NS], T.kd[:, 0::NS], float(O * H), None, ALU.add))
+    v(V.tensor_scalar(T.b3[:], T.kd[:, 1:4 * NS:NS], T.pm[:, 0:1], float(NS), ALU.add, ALU.mult))
     v(V.tensor_scalar(T.idn[:], T.dia[:], 0.0, -1.0, ALU.is_equal, ALU.mult))
-    v(V.tensor_scalar(T.idp[:], T.dia[:], 0.0, None, ALU.is_equal))
-    vwait(a)
-    v(V.tensor_scalar(T.b3[:], T.b40[:, 0:4], 64.0, 4.0 * (KC - 1), ALU.mult, ALU.min))
-    consts = v(V.tensor_scalar(T.pe[:], T.px[:], T.pm[:, 2:3], None, ALU.add))
-    V.wait_ge(sem.ldl, 16)
-    last = v(V.tensor_copy(T.lu[:, 0:LC], T.li[:, 0:LC]))
+    consts = v(V.tensor_scalar(T.idp[:], T.dia[:], 0.0, None, ALU.is_equal))
+    vwait(consts)
+    v(V.tensor_scalar(T.b3[:], T.b3[:], 1.0, None, ALU.add))
+    for c0 in (KC * NS, LX + KC * NS):
+        v(V.tensor_scalar(T.lx[:, c0:c0 + LX - KC * NS], T.kd[:], T.pm[:, 0:1], None, ALU.add))
+    lists_wait(0)
+    offsets(0, 1)
+    last = offsets(0, 0)
+    for i in range(3):
+        table(0, i)
     V.wait_ge(sem.ldr, 16)
     S.wait_ge(sem.ldr, 16)
     P.wait_ge(sem.vs, consts)
-    P.wait_ge(sem.gs, block)
-    copied = 0
-    parts = [(0, BANK), (BANK, K)]
+    free_s = free_v = e = 0
 
     for t in range(M):
         R = T.rb if t == 0 else T.rf
-        bt = T.bb[:, t * K:(t + 1) * K]
 
-        def way(o):
-            return R[:, 0:W].indirect(T.lu[:, t * LC + o * KC:t * LC + (o + 1) * KC])
+        def on(o0, o1, h):
+            c0 = t * LC + h * O * HC
+            return R[:, 0:W].indirect(T.lu[:, c0 + o0 * HC:c0 + o1 * HC])
 
-        def sum_abs(o, src):
-            return mark(S.activation(T.ab[:, o * K:(o + 1) * K], src, ACT.Abs, accum_out=T.acc[:, 3 - o:4 - o]), "ss")
+        def elected(win):
+            return win[:].indirect(T.lw[:, KC:KC + HC])
+
+        def bank(o):
+            return T.pd[:, o * BANK:o * BANK + H]
+
+        def part(buf, o):
+            return buf[:, o * H:(o + 1) * H]
 
         S.wait_ge(sem.vs, last)
-        s3 = mark(S.activation(T.r3[:], way(3), ACT.Identity), "ss")
+        sa = s(S.activation(T.rs[:, 2 * H:4 * H], on(2, 4, 1), ACT.Identity))
+        sb = s(S.activation(T.rs[:, 0:2 * H], on(0, 2, 1), ACT.Identity))
         frame_wait(P, t)
-        if copied:
-            P.wait_ge(sem.ss, copied)
-        for a0, a1 in parts:
-            P.matmul(T.pd[:, a0:a1], T.idn[:], T.bb[:, t * K + a0:t * K + a1], True, False)
-        P.wait_ge(sem.ss, s3)
-        for a0, a1 in parts:
-            p3 = mark(P.matmul(T.pd[:, a0:a1], T.idp[:], T.r3[:, a0:a1], False, True), "ps")
-        P.matmul(T.key[:, 0:O], T.blk[:], T.mid[:], True, False)
+        if t:
+            P.wait_ge(sem.ss, free_s)
+            P.wait_ge(sem.vs, free_v)
+        for o in (3, 2, 1, 0):
+            P.matmul(bank(o), T.idn[:], T.bb[:, t * K + H:(t + 1) * K], True, False)
+        if t:
+            P.wait_ge(sem.vs, e)
+        else:
+            P.wait_ge(sem.gs, block)
+        P.matmul(T.key[:, 0:8], T.blk[:], T.mid[:], True, False)
+        pp = {}
+        P.wait_ge(sem.ss, sa)
+        for o in (3, 2):
+            pp[o] = mark(P.matmul(bank(o), T.idp[:], part(T.rs, o), False, True), "ps")
+        P.wait_ge(sem.ss, sb)
+        for o in (1, 0):
+            pp[o] = mark(P.matmul(bank(o), T.idp[:], part(T.rs, o), False, True), "ps")
+        table(t, 3)
         frame_wait(V, t)
         vwait(last)
-        gk = {o: v(V.tensor_tensor(T.dd[:, o * K:(o + 1) * K], way(o), bt, ALU.subtract)) for o in (2, 1, 0)}
-        S.wait_ge(sem.vs, gk[2])
-        sum_abs(2, T.dd[:, 2 * K:3 * K])
-        S.wait_ge(sem.ps, p3)
-        sum_abs(3, T.pd[:, 0:K])
-        S.wait_ge(sem.vs, gk[1])
-        s1 = sum_abs(1, T.dd[:, K:2 * K])
-        copied = mark(S.activation(T.dd[:, 3 * K:4 * K], T.pd[:, 0:K], ACT.Identity), "ss")
-        vwait(gk[0])
-        rv = v(V.tensor_reduce(T.acc[:, 3:4], T.dd[:, 0:K], AX.X, ALU.add, apply_absolute_value=True))
+        gk = {o: v(V.tensor_tensor(part(T.dd, o), on(o, o + 1, 0), T.bb[:, t * K:t * K + H], ALU.subtract)) for o in (3, 2, 1, 0)}
+        for o in (3, 2):
+            S.wait_ge(sem.vs, gk[o])
+            s1 = s(S.activation(part(T.ab, o), part(T.dd, o), ACT.Abs, accum_out=T.ac1[:, 3 - o:4 - o]))
+        for o in (3, 2):
+            S.wait_ge(sem.ps, pp[o])
+            s2 = s(S.activation(part(T.ab, o - 2), bank(o), ACT.Abs, accum_out=T.ac2[:, 3 - o:4 - o]))
+        for o in (1, 0):
+            vwait(gk[o])
+            v1 = v(V.tensor_reduce(T.ac1[:, 3 - o:4 - o], part(T.dd, o), AX.X, ALU.add, apply_absolute_value=True))
+        for o in (1, 0):
+            V.wait_ge(sem.ps, pp[o])
+            v2 = v(V.tensor_reduce(T.ac2[:, 3 - o:4 - o], bank(o), AX.X, ALU.add, apply_absolute_value=True))
         P.wait_ge(sem.ss, s1)
-        P.wait_ge(sem.vs, rv)
-        pk = mark(P.matmul(T.key[:, 0:O], T.blk[:], T.acc[:], False, True), "ps")
-        v(V.tensor_copy(T.lx[:], T.li[:, t * LC:(t + 1) * LC].indirect(T.pe[:, 0:LC // 16])))
-        if t + 1 < M:
-            if t == 0:
-                V.wait_ge(sem.ldl2, 16)
-            elif t + 1 >= F:
-                V.wait_ge(sem["al%d" % (t + 1)], arrivals(t + 1))
-            v(V.tensor_copy(T.lu[:, (t + 1) * LC:(t + 2) * LC], T.li[:, (t + 1) * LC:(t + 2) * LC]))
+        P.wait_ge(sem.vs, v1)
+        P.matmul(T.key[:, 0:8], T.blk[:], T.ac1[:], False, False)
+        P.wait_ge(sem.ss, s2)
+        P.wait_ge(sem.vs, v2)
+        pk = mark(P.matmul(T.key[:, 0:8], T.blk[:], T.ac2[:], False, True), "ps")
+        free_v = v(V.tensor_scalar(part(T.t1, 0), bank(0), float(C), 0.0, ALU.add, ALU.max))
+        table(t, 4)
+        for o in (3, 2):
+            s(S.activation(part(T.t1, o), bank(o), ACT.Relu, bias=float(C)))
+        S.wait_ge(sem.vs, v2 - 1)
+        s(S.activation(T.t1[:, H + LATE:2 * H], T.pd[:, BANK + LATE:BANK + H], ACT.Relu, bias=float(C)))
         V.wait_ge(sem.ps, pk)
-        v(V.tensor_tensor_scan(T.m1[:], T.one[:], T.key[:, 0:O], 1.0e9, ALU.add, ALU.min))
-        a = v(V.tensor_reduce(T.mn[:, 0:1], T.key[:, 0:O], AX.X, ALU.min))
+        a = v(V.tensor_tensor_scan(T.m1[:, 0:7], T.one[:, 0:7], T.key[:, 0:7], 1.0e9, ALU.add, ALU.min))
+        if t + 1 < M:
+            lists_wait(t + 1)
+        offsets(t + 1, 1)
         vwait(a)
-        a = v(V.tensor_scalar(T.o3[:, 0:3], T.b3[:, 0:3], T.m1[:, 3:4], T.mn[:, 0:1], ALU.add, ALU.subtract))
-        b = v(V.tensor_scalar(T.w40[:, 0:1], T.m1[:, 3:4], T.mn[:, 0:1], float(KC), ALU.subtract, ALU.mult))
+        a = v(V.tensor_scalar(T.o3[:, 0:4], T.b3[:], T.m1[:, 3:4], T.m1[:, 6:7], ALU.add, ALU.subtract))
+        offsets(t + 1, 0)
         vwait(a)
-        e = v(V.tensor_copy(T.lw[:], T.lx[:, 0:LC].indirect(T.o3[:, 0:3])))
-        vwait(b)
-        a = v(V.tensor_scalar(T.o40[:], T.b40[:], T.w40[:, 0:1], 16.0, ALU.add, ALU.mult))
-        vwait(a)
-        V.wait_ge(sem.ss, copied)
-        a = v(V.tensor_scalar(T.cc[:], T.dd[:, 0:O * K].indirect(T.o40[:, 0:KC]), float(-C), float(C), ALU.max, ALU.min))
+        e = v(V.tensor_copy(T.lw[:], T.lx[:, t % 2 * LX:(t % 2 + 1) * LX].indirect(T.o3[:, 0:4])))
+        table(t + 1, 0)
+        final = t == M - 1
+        rr, cc, new = (T.rq, T.cq, T.rb) if final else (T.rr, T.cc, T.rf)
+        vwait(e)
+        if final:
+            a = v(V.tensor_scalar(T.tq[:], elected(T.dd), -1.0, float(C), ALU.mult, ALU.min))
+            vwait(a)
+            a = v(V.tensor_scalar(cc[:, 0:H], T.tq[:], float(-C), None, ALU.max))
+        else:
+            a = v(V.tensor_scalar(cc[:, 0:H], elected(T.dd), float(-C), float(C), ALU.max, ALU.min))
+        table(t + 1, 1)
         S.wait_ge(sem.vs, e)
-        sr = mark(S.activation(T.rr[:], R[:, 0:W].indirect(T.lw[:, 0:KC]), ACT.Identity), "ss")
-        if t == 0:
-            V.wait_ge(sem.cast, 16)
+        sr = s(S.activation(rr[:, 0:H], R[:, 0:W].indirect(T.lw[:, 0:HC]), ACT.Identity))
+        free_s = s(S.activation(T.t1[:, H:H + LATE], T.pd[:, BANK:BANK + LATE], ACT.Relu, bias=float(C)))
+        s(S.activation(rr[:, H:K], elected(T.rs), ACT.Identity, bias=0.0 if final else float(-C)))
+        S.wait_ge(sem.ss, free_s)
+        st = s(S.activation(T.cc[:, H:K], elected(T.t1), ACT.Relu, bias=float(2 * C), scale=-1.0))
+        if final:
+            S.wait_ge(sem.ss, st)
+            st = s(S.activation(cc[:, H:K], T.cc[:, H:K], ACT.Identity, bias=float(-C)))
+        if t == 0 or final:
+            V.wait_ge(sem.cast, 32 if final else 16)
+            V.wait_ge(sem.wide, 2 if final else 1)
         vwait(a)
         V.wait_ge(sem.ss, sr)
-        last = v(V.tensor_tensor(T.rf[:, 0:W].indirect(T.lw[:, 0:KC]), T.rr[:], T.cc[:], ALU.subtract))
+        a = v(V.tensor_tensor(new[:, 0:W].indirect(T.lw[:, 0:HC]), rr[:, 0:H], cc[:, 0:H], ALU.add if final else ALU.subtract))
+        table(t + 1, 2)
+        vwait(a)
+        V.wait_ge(sem.ss, st)
+        before, last = last, v(V.tensor_tensor(new[:, 0:W].indirect(T.lw[:, HC:KC]), rr[:, H:K], cc[:, H:K], ALU.add))
 
     g.wait_ge(sem.sent, sent)
     g.wait_ge(sem.fed, fed)
-    g.wait_ge(sem.vs, last)
-    g.dma_start(T.y[:], T.rf[:]).then_inc(sem.stored, 16)
-    g.wait_ge(sem.stored, 16)
+    g.wait_ge(sem.vs, before)
+    g.dma_start(T.rb[:, GW:W], T.rf[:, GW:W]).then_inc(sem.cast, 16)
+    g.affine_select(T.rb[:, 0:GW], T.rf[:, 0:GW], [[0, GW]], ALU.is_ge, 0.0, 0, 0).then_inc(sem.wide, 1)
+    Y.wait_ge(sem.vs, last)
+    Y.dma_start(T.y[:], T.rb[:]).then_inc(sem.stored, 16)
+    Y.wait_ge(sem.stored, 16)

from concourse.mybir import AluOpType as ALU, AxisListType as AX, ActivationFunctionType as ACT

N, W, K, F, O, C = 4, 2048, 640, 3, 4, 8
KC = K // 16
LC = O * KC
M = N * F
BANK = 512
H = K // 2
HC = H // 16
SLOTS = [3, 0, 1, 2, 3]
NS = len(SLOTS)
LW = 64
LX = LW * NS
LATE = 96
GW = 1280
BIG = 3.0 * 2 ** 24
MID = -160000.0

SCRATCH = {
    "rb": ("sbuf", [128, W], "bfloat16"),
    "rf": ("sbuf", [128, W], "float32"),
    "bb": ("sbuf", [128, M * K], "bfloat16"),
    "li": ("sbuf", [128, M * O, KC], "int32"),
    "lu": ("sbuf", [128, M * LC], "uint16"),
    "lx": ("sbuf", [128, 2 * LX], "int32"),
    "so": ("sbuf", [128, M * K], "bfloat16"),
    "sl": ("sbuf", [128, M * O, KC], "int32"),
    "dd": ("sbuf", [128, O * H], "float32"),
    "rs": ("sbuf", [128, O * H], "bfloat16"),
    "t1": ("sbuf", [128, O * H], "float32"),
    "ab": ("sbuf", [128, O * H], "float32"),
    "rr": ("sbuf", [128, K], "float32"),
    "cc": ("sbuf", [128, K], "float32"),
    "rq": ("sbuf", [128, K], "bfloat16"),
    "cq": ("sbuf", [128, K], "bfloat16"),
    "tq": ("sbuf", [128, H], "bfloat16"),
    "ac1": ("sbuf", [128, 8], "float32"),
    "ac2": ("sbuf", [128, 8], "float32"),
    "m1": ("sbuf", [128, 8], "float32"),
    "o3": ("sbuf", [128, 8], "uint16"),
    "lw": ("sbuf", [128, LW], "uint16"),
    "pi": ("sbuf", [128, 4], "int32"),
    "pj": ("sbuf", [128, 4], "int32"),
    "pm": ("sbuf", [128, 4], "float32"),
    "kd": ("sbuf", [128, LX - KC * NS], "float32"),
    "b3": ("sbuf", [128, 4], "float32"),
    "one": ("sbuf", [128, 8], "float32"),
    "mid": ("sbuf", [128, 8], "float32"),
    "dia": ("sbuf", [128, 128], "float32"),
    "blk": ("sbuf", [128, 128], "float32"),
    "idp": ("sbuf", [128, 128], "bfloat16"),
    "idn": ("sbuf", [128, 128], "bfloat16"),
    "pd": ("psum", [128, O * BANK], "float32"),
    "key": ("psum", [128, BANK], "float32"),
}
STAGES = [(F, F + 1), (F + 1, 2 * F)] + [(d * F, (d + 1) * F) for d in range(2, N)]
RELAYED = list(range(F + 1, M, 2))
SEMAPHORES = (["vs", "ss", "ps", "gs", "ldr", "ldl", "ldb", "ldl2", "ldb1", "ldb2", "cast", "wide", "sent", "fed", "stored"]
              + ["st%d" % i for i in range(len(STAGES))]
              + ["al%d" % t for t in range(F, M)]
              + ["ao%d" % t for t in range(F, M)]
              + ["hp%d" % t for t in RELAYED])


def helper_of(c, T, topo):
    for h in topo.cores_of(c):
        if topo.die(h) != topo.die(c) and h not in T.cores and all(topo.may_write(h, r) for r in T.cores if r != c):
            return h


def feed_engines(c, T, topo):
    off = [e for r in T.cores if r != c for e in topo.engines(c, r)]
    return [e for e in topo.engines(c, helper_of(c, T, topo)) if e not in off]


def send_unit(g, T, topo, src, dst, t, to_l, to_o, sem_l, sem_o, local, engines):
    rid, pid, _ = topo.addr(dst)
    mask = sum(1 << e for e in engines)
    g.remote_dma(to_l[:, t * O:(t + 1) * O], T.sl[:, t * O:(t + 1) * O], sem_l, local, pid, rid, mask)
    g.remote_dma(to_o[:, t * K:(t + 1) * K], T.so[:, t * K:(t + 1) * K], sem_o, local, pid, rid, mask)
    return 2 * len(engines)


def helper_program(g, core, owner, T, topo):
    rank, sent = T.rank_of(owner), 0
    for t in RELAYED:
        dst = T.cores[(rank - t // F) % N]
        g.wait_ge(T.sem["hp%d" % t], 2 * len(feed_engines(owner, T, topo)))
        if sent:
            g.wait_ge(T.sem.sent, sent)
        sent += send_unit(g, T, topo, core, dst, t, T.li, T.bb, T.sem["al%d" % t], T.sem["ao%d" % t], T.sem.sent,
                          topo.engines(core, dst))
    g.wait_ge(T.sem.sent, sent)


def rank_program(g, core, T, topo):
    rank = T.rank_of(core)
    if rank is None:
        for c in T.cores:
            if helper_of(c, T, topo) == core:
                helper_program(g, core, c, T, topo)
        return
    V, S, P, Y, sem = g.vector, g.scalar, g.tensor, g.sync, T.sem
    n = {"vs": 0, "ss": 0, "ps": 0, "gs": 0}

    def mark(ins, name):
        ins.then_inc(sem[name], 1)
        n[name] += 1
        return n[name]

    def v(ins):
        return mark(ins, "vs")

    def s(ins):
        return mark(ins, "ss")

    def vwait(k):
        V.wait_ge(sem.vs, k)

    ob, ol = rank * F * K, rank * F * LC

    Y.dma_start(T.rb[:], T.ref0[:]).then_inc(sem.ldr, 16)
    S.dma_start(T.li[:, 0:O], T.ops[:, ol:ol + LC]).then_inc(sem.ldl, 16)
    S.dma_start(T.bb[:, 0:K], T.obs[:, ob:ob + K]).then_inc(sem.ldb, 16)
    Y.wait_ge(sem.ldr, 16)
    Y.dma_start(T.bb[:, K:2 * K], T.obs[:, ob + K:ob + 2 * K]).then_inc(sem.ldb1, 16)
    for i, (t0, t1) in enumerate(STAGES):
        d = t0 // F
        u = ((rank - d) % N - d) * F
        Y.dma_start(T.sl[:, t0 * O:t1 * O], T.ops[:, (u + t0) * LC:(u + t1) * LC]).then_inc(sem["st%d" % i], 16)
        Y.dma_start(T.so[:, t0 * K:t1 * K], T.obs[:, (u + t0) * K:(u + t1) * K]).then_inc(sem["st%d" % i], 16)
        if i == 0:
            Y.dma_start(T.bb[:, 2 * K:F * K], T.obs[:, ob + 2 * K:ob + F * K]).then_inc(sem.ldb2, 16)
        if i < len(STAGES) - 1:
            Y.wait_ge(sem["st%d" % i], 32)

    mark(g.iota(T.pi[:, 0:1], [[0, 1]], 0, 1), "gs")
    mark(g.iota(T.kd[:], [[16, LW - KC], [H, NS]], -H, 0, allow_small_or_imprecise_dtypes=True), "gs")
    mark(g.iota(T.dia[:], [[-1, 128]], 0, 1, allow_small_or_imprecise_dtypes=True), "gs")
    a = mark(g.iota(T.blk[:], [[0, 128]], 4, 0, allow_small_or_imprecise_dtypes=True), "gs")
    g.dma_start(T.li[:, O:F * O], T.ops[:, ol + LC:ol + F * LC]).then_inc(sem.ldl2, 16)
    g.wait_ge(sem.gs, a)
    a = mark(g.affine_select(T.blk[:], T.blk[:], [[16, 8], [0, 16]], ALU.is_gt, 0.0, 16, -1), "gs")
    g.wait_ge(sem.gs, a)
    block = mark(g.affine_select(T.blk[:], T.blk[:], [[-16, 8], [0, 16]], ALU.is_ge, 0.0, 0, 1), "gs")
    g.dma_start(T.rf[:, GW:W], T.ref0[:, GW:W]).then_inc(sem.cast, 16)
    g.wait_ge(sem.ldr, 16)
    g.affine_select(T.rf[:, 0:GW], T.rb[:, 0:GW], [[0, GW]], ALU.is_ge, 0.0, 0, 0).then_inc(sem.wide, 1)
    helper = helper_of(core, T, topo)
    sent = fed = 0
    for i, (t0, t1) in enumerate(STAGES):
        g.wait_ge(sem["st%d" % i], 32)
        for t in range(t0, t1):
            if t in RELAYED:
                fed += send_unit(g, T, topo, core, helper, t, T.sl, T.so, sem["hp%d" % t], sem["hp%d" % t], sem.fed,
                                 feed_engines(core, T, topo))
        for t in range(t0, t1):
            if t not in RELAYED:
                dst = T.cores[(rank - t // F) % N]
                if sent:
                    g.wait_ge(sem.sent, sent)
                sent += send_unit(g, T, topo, core, dst, t, T.li, T.bb, sem["al%d" % t], sem["ao%d" % t], sem.sent,
                                  topo.engines(core, dst))

    def arrivals(t):
        src = T.cores[(rank + t // F) % N]
        return len(topo.engines(helper_of(src, T, topo) if t in RELAYED else src, core))

    def frame_wait(Q, t):
        if t < F:
            Q.wait_ge(sem[("ldb", "ldb1", "ldb2")[t]], 16)
        else:
            Q.wait_ge(sem["ao%d" % t], arrivals(t))

    def lists_wait(t):
        if t < 2:
            V.wait_ge(sem[("ldl", "ldl2")[t]], 16)
        elif t >= F:
            V.wait_ge(sem["al%d" % t], arrivals(t))

    def offsets(t, h):
        if t < M:
            c0 = t * LC + h * O * HC
            return v(V.tensor_copy(T.lu[:, c0:c0 + O * HC], T.li[:, t * O:(t + 1) * O, h * HC:(h + 1) * HC]))

    def table(t, i):
        if t < M:
            c0 = t % 2 * LX
            return v(V.tensor_copy(T.lx[:, c0 + i:c0 + KC * NS:NS], T.li[:, t * O + SLOTS[i]]))

    for c0, c1, step in ((0, 4, 1.0), (4, 5, -1.0), (5, 6, BIG), (6, 8, -BIG)):
        v(V.memset(T.one[:, c0:c1], step))
    v(V.memset(T.mid[:, 0:4], MID))
    v(V.memset(T.mid[:, 4:8], BIG))
    v(V.memset(T.ac1[:], 0.0))
    v(V.memset(T.ac2[:], 0.0))
    V.wait_ge(sem.gs, 1)
    a = v(V.tensor_scalar(T.pj[:, 0:1], T.pi[:, 0:1], 15, None, ALU.bitwise_and))
    vwait(a)
    a = v(V.tensor_copy(T.pm[:, 0:1], T.pj[:, 0:1]))
    vwait(a)
    V.wait_ge(sem.gs, 3)
    v(V.tensor_scalar(T.kd[:, 0::NS], T.kd[:, 0::NS], float(O * H), None, ALU.add))
    v(V.tensor_scalar(T.b3[:], T.kd[:, 1:4 * NS:NS], T.pm[:, 0:1], float(NS), ALU.add, ALU.mult))
    v(V.tensor_scalar(T.idn[:], T.dia[:], 0.0, -1.0, ALU.is_equal, ALU.mult))
    consts = v(V.tensor_scalar(T.idp[:], T.dia[:], 0.0, None, ALU.is_equal))
    vwait(consts)
    v(V.tensor_scalar(T.b3[:], T.b3[:], 1.0, None, ALU.add))
    for c0 in (KC * NS, LX + KC * NS):
        v(V.tensor_scalar(T.lx[:, c0:c0 + LX - KC * NS], T.kd[:], T.pm[:, 0:1], None, ALU.add))
    lists_wait(0)
    offsets(0, 1)
    last = offsets(0, 0)
    for i in range(3):
        table(0, i)
    V.wait_ge(sem.ldr, 16)
    S.wait_ge(sem.ldr, 16)
    P.wait_ge(sem.vs, consts)
    free_s = free_v = e = 0

    for t in range(M):
        R = T.rb if t == 0 else T.rf

        def on(o0, o1, h):
            c0 = t * LC + h * O * HC
            return R[:, 0:W].indirect(T.lu[:, c0 + o0 * HC:c0 + o1 * HC])

        def elected(win):
            return win[:].indirect(T.lw[:, KC:KC + HC])

        def bank(o):
            return T.pd[:, o * BANK:o * BANK + H]

        def part(buf, o):
            return buf[:, o * H:(o + 1) * H]

        S.wait_ge(sem.vs, last)
        sa = s(S.activation(T.rs[:, 2 * H:4 * H], on(2, 4, 1), ACT.Identity))
        sb = s(S.activation(T.rs[:, 0:2 * H], on(0, 2, 1), ACT.Identity))
        frame_wait(P, t)
        if t:
            P.wait_ge(sem.ss, free_s)
            P.wait_ge(sem.vs, free_v)
        for o in (3, 2, 1, 0):
            P.matmul(bank(o), T.idn[:], T.bb[:, t * K + H:(t + 1) * K], True, False)
        if t:
            P.wait_ge(sem.vs, e)
        else:
            P.wait_ge(sem.gs, block)
        P.matmul(T.key[:, 0:8], T.blk[:], T.mid[:], True, False)
        pp = {}
        P.wait_ge(sem.ss, sa)
        for o in (3, 2):
            pp[o] = mark(P.matmul(bank(o), T.idp[:], part(T.rs, o), False, True), "ps")
        P.wait_ge(sem.ss, sb)
        for o in (1, 0):
            pp[o] = mark(P.matmul(bank(o), T.idp[:], part(T.rs, o), False, True), "ps")
        table(t, 3)
        frame_wait(V, t)
        vwait(last)
        gk = {o: v(V.tensor_tensor(part(T.dd, o), on(o, o + 1, 0), T.bb[:, t * K:t * K + H], ALU.subtract)) for o in (3, 2, 1, 0)}
        for o in (3, 2):
            S.wait_ge(sem.vs, gk[o])
            s1 = s(S.activation(part(T.ab, o), part(T.dd, o), ACT.Abs, accum_out=T.ac1[:, 3 - o:4 - o]))
        for o in (3, 2):
            S.wait_ge(sem.ps, pp[o])
            s2 = s(S.activation(part(T.ab, o - 2), bank(o), ACT.Abs, accum_out=T.ac2[:, 3 - o:4 - o]))
        for o in (1, 0):
            vwait(gk[o])
            v1 = v(V.tensor_reduce(T.ac1[:, 3 - o:4 - o], part(T.dd, o), AX.X, ALU.add, apply_absolute_value=True))
        for o in (1, 0):
            V.wait_ge(sem.ps, pp[o])
            v2 = v(V.tensor_reduce(T.ac2[:, 3 - o:4 - o], bank(o), AX.X, ALU.add, apply_absolute_value=True))
        P.wait_ge(sem.ss, s1)
        P.wait_ge(sem.vs, v1)
        P.matmul(T.key[:, 0:8], T.blk[:], T.ac1[:], False, False)
        P.wait_ge(sem.ss, s2)
        P.wait_ge(sem.vs, v2)
        pk = mark(P.matmul(T.key[:, 0:8], T.blk[:], T.ac2[:], False, True), "ps")
        free_v = v(V.tensor_scalar(part(T.t1, 0), bank(0), float(C), 0.0, ALU.add, ALU.max))
        table(t, 4)
        for o in (3, 2):
            s(S.activation(part(T.t1, o), bank(o), ACT.Relu, bias=float(C)))
        S.wait_ge(sem.vs, v2 - 1)
        s(S.activation(T.t1[:, H + LATE:2 * H], T.pd[:, BANK + LATE:BANK + H], ACT.Relu, bias=float(C)))
        V.wait_ge(sem.ps, pk)
        a = v(V.tensor_tensor_scan(T.m1[:, 0:7], T.one[:, 0:7], T.key[:, 0:7], 1.0e9, ALU.add, ALU.min))
        if t + 1 < M:
            lists_wait(t + 1)
        offsets(t + 1, 1)
        vwait(a)
        a = v(V.tensor_scalar(T.o3[:, 0:4], T.b3[:], T.m1[:, 3:4], T.m1[:, 6:7], ALU.add, ALU.subtract))
        offsets(t + 1, 0)
        vwait(a)
        e = v(V.tensor_copy(T.lw[:], T.lx[:, t % 2 * LX:(t % 2 + 1) * LX].indirect(T.o3[:, 0:4])))
        table(t + 1, 0)
        final = t == M - 1
        rr, cc, new = (T.rq, T.cq, T.rb) if final else (T.rr, T.cc, T.rf)
        vwait(e)
        if final:
            a = v(V.tensor_scalar(T.tq[:], elected(T.dd), -1.0, float(C), ALU.mult, ALU.min))
            vwait(a)
            a = v(V.tensor_scalar(cc[:, 0:H], T.tq[:], float(-C), None, ALU.max))
        else:
            a = v(V.tensor_scalar(cc[:, 0:H], elected(T.dd), float(-C), float(C), ALU.max, ALU.min))
        table(t + 1, 1)
        S.wait_ge(sem.vs, e)
        sr = s(S.activation(rr[:, 0:H], R[:, 0:W].indirect(T.lw[:, 0:HC]), ACT.Identity))
        free_s = s(S.activation(T.t1[:, H:H + LATE], T.pd[:, BANK:BANK + LATE], ACT.Relu, bias=float(C)))
        s(S.activation(rr[:, H:K], elected(T.rs), ACT.Identity, bias=0.0 if final else float(-C)))
        S.wait_ge(sem.ss, free_s)
        st = s(S.activation(T.cc[:, H:K], elected(T.t1), ACT.Relu, bias=float(2 * C), scale=-1.0))
        if final:
            S.wait_ge(sem.ss, st)
            st = s(S.activation(cc[:, H:K], T.cc[:, H:K], ACT.Identity, bias=float(-C)))
        if t == 0 or final:
            V.wait_ge(sem.cast, 32 if final else 16)
            V.wait_ge(sem.wide, 2 if final else 1)
        vwait(a)
        V.wait_ge(sem.ss, sr)
        a = v(V.tensor_tensor(new[:, 0:W].indirect(T.lw[:, 0:HC]), rr[:, 0:H], cc[:, 0:H], ALU.add if final else ALU.subtract))
        table(t + 1, 2)
        vwait(a)
        V.wait_ge(sem.ss, st)
        before, last = last, v(V.tensor_tensor(new[:, 0:W].indirect(T.lw[:, HC:KC]), rr[:, H:K], cc[:, H:K], ALU.add))

    g.wait_ge(sem.sent, sent)
    g.wait_ge(sem.fed, fed)
    g.wait_ge(sem.vs, before)
    g.dma_start(T.rb[:, GW:W], T.rf[:, GW:W]).then_inc(sem.cast, 16)
    g.affine_select(T.rb[:, 0:GW], T.rf[:, 0:GW], [[0, GW]], ALU.is_ge, 0.0, 0, 0).then_inc(sem.wide, 1)
    Y.wait_ge(sem.vs, last)
    Y.dma_start(T.y[:], T.rb[:]).then_inc(sem.stored, 16)
    Y.wait_ge(sem.stored, 16)
